import numpy as np, ml_dtypes
CORES = [23,119,17,113]
N = 4
BF = ml_dtypes.bfloat16
def gentries(a):
    return np.ascontiguousarray(a.reshape(8, 16, -1).transpose(0, 2, 1)).reshape(8, -1)
def gtable(e):
    e = np.asarray(e); return np.ascontiguousarray(e.reshape(8, -1, 16).transpose(0, 2, 1)).reshape(128, -1).astype(np.int32)
W, E, P = 2560, 896, 5
M = (P - 1) // 2
def lens(rng, n, rw, how):
    i = np.arange(n)
    if how == 0: v = i % (P + 1)
    elif how == 1: v = np.where(i < (W - n - rw * (2 + M)) // ((P + 1) // 2), P, 0)
    elif how == 2: v = np.where(i % 10 < 9, 0, 1 + (i // 10) % P)
    elif how == 3: v = i % 3
    else: v = np.full(n, 1)
    return rng.permutation(v)
def colours(rng, ln, lo, hi):
    n = len(ln); a = rng.integers(lo, hi, n); b = lo + (a - lo + rng.integers(1, hi - lo, n)) % (hi - lo)
    x, y = np.maximum(a, b), np.minimum(a, b); z = ln == 0; same = rng.random(n) < 0.5
    return np.where(z, x, a), np.where(z, np.where(same, x, y), b)
def special(rng, rw):
    kd = (np.arange(rw) + rng.integers(0, 7)) % 7; q = rng.random(rw) < 0.5
    s = np.sort(np.argsort(rng.random((rw, 16)), axis=1)[:, :3], axis=1); j = rng.integers(0, 3, rw)
    j = np.where(kd == 0, 2, np.where((kd == 1) | (kd == 5), j % 2, j))
    s = np.take_along_axis(s, np.array([[2, 0, 1], [1, 0, 2], [0, 1, 2]])[j], axis=1)
    add, mul, span = np.array([[2, 2, 1, 1, 3, 0, 2], [2, 1, 2, 1, 1, 1, 1], [M, 1, 2, 4, 2, 1, 3]])[:, kd]
    return kd, q, s[:, 0], s[:, 1], s[:, 2], add + mul * (span * rng.random(rw)).astype(np.int64)
def way(v, ln, pl, pr):
    X = np.full((len(ln), P + 1), -1); X[:, 0] = v
    for i in range(1, P + 1):
        m = ln >= i; n = int(np.count_nonzero(m))
        if i % 2: X[m, i] = pl[:n]; pl = pl[n:]
        else: X[m, i] = pr[:n]; pr = pr[n:]
    return X, pl, pr
def plant(LT, RT, X, ln, a, b):
    for i in range(1, P + 1):
        m = ln >= i; p, x = X[m, i - 1], X[m, i]
        if i % 2: c = a[m]; RT[c, p] = x; LT[c, x] = p
        else: c = b[m]; LT[c, p] = x; RT[c, x] = p
    e = X[np.arange(len(ln)), ln]; m = ln % 2 == 0
    RT[a[m], e[m]] = -1; LT[b[~m], e[~m]] = -1
def graph(rng, rw, H, how, drop, order):
    LT = np.full((16, W), -2); RT = np.full((16, W), -2); LM = np.zeros((16, W), bool); RM = np.zeros((16, W), bool)
    C = np.arange(16)[:, None]; F = E - rw; S = E // 8
    if order == 0: nl, nr = rng.permutation(W), rng.permutation(W)
    elif order == 1: nl, nr = np.arange(W), np.arange(W)
    else: nl, nr = np.arange(W)[::-1], np.arange(W)[::-1]
    kd, q, a0, b0, e, l0 = special(rng, rw)
    ln = np.concatenate([l0, lens(rng, F, rw, how)])
    a, b = colours(rng, ln, 0, H); a[:rw] = a0; b[:rw] = b0
    u, v = nl[:E], nr[:E]; X, zl, zr = way(v, ln, nl[E:], nr[E:])
    plant(LT, RT, X, ln, a, b)
    LT[a, u] = -1; RT[b, v] = -1; LM[:, u] = C < a; RM[:, v] = C < b
    u0, v0, Z = u[:rw], v[:rw], X[:rw]; end = Z[np.arange(rw), l0]
    ua, zl = zl[:rw], zl[rw:]; zz, zr = zr[:rw], zr[rw:]
    m = (kd == 5) & q; n = int(np.count_nonzero(m)); p = np.array(ua); p[m] = zl[:n]; zl = zl[n:]
    c = np.where((kd == 3) | ((kd == 4) & q), b0, np.where(m | (kd == 6), e, a0))
    d = np.where((kd >= 2) & (kd <= 4), e, np.where((kd == 6) & q, a0, b0))
    y = np.where(kd < 2, end, np.where(kd == 4, Z[:, 2], np.where(kd == 6, zz, v0))); u1 = np.where(kd == 2, end, ua)
    s = np.where(kd == 3, Z[:, 1], np.where(kd == 4, np.where(q, Z[:, 3], Z[:, 1]), np.where(m, p, u0)))
    LM[:, u1] = C < c; RM[:, y] = C < d
    i = kd != 2; LT[c[i], ua[i]] = -1
    i = kd > 1; RT[d[i], y[i]] = -1
    i = (kd > 0) & (kd < 6); LT[d[i], s[i]] = zz[i]; RT[d[i], zz[i]] = s[i]; RT[c[i], zz[i]] = -1
    RT[e[m], v0[m]] = p[m]; LT[e[m], p[m]] = v0[m]
    i = kd == 6; x = Z[i, 1]; RT[e[i], zz[i]] = x; LT[e[i], x] = zz[i]; RT[e[i], np.where(q, Z[:, 2], v0)[i]] = -1
    i = kd == 0; LT[b0[i], u0[i]] = -1
    pu = rng.permutation(np.concatenate([u[rw:], zl[:S]])); pv = rng.permutation(np.concatenate([v[rw:], zr[:S]]))
    u2, v2 = pu[:F], pv[:F]; tl, tr = X[rw:, 1::2], X[rw:, 2::2]
    restl = rng.permutation(np.concatenate([pu[F:], zl[S:], tl[tl >= 0]])); restr = rng.permutation(np.concatenate([pv[F:], zr[S:], tr[tr >= 0]]))
    still = np.zeros(W, bool); still[v[(ln == 0) & (a > b)]] = True; z = still[v2]; g = ~z
    l2 = lens(rng, F, rw, how); l2[z] = 0
    c, d = colours(rng, l2, H, 16); Y, _, _ = way(v2, l2, restl, restr)
    plant(LT, RT, Y, l2, c, d)
    LT[c, u2] = -1; LM[:, u2] = LM[:, u2] | (C < c)
    RT[d[g], v2[g]] = -1; RM[:, v2[g]] = RM[:, v2[g]] | (C < d[g])
    for k in range(16):
        x, w = np.flatnonzero(LT[k] == -2), np.flatnonzero(RT[k] == -2); n = min(len(x), len(w))
        x = x[np.argsort(rng.random(len(x)) - 2.0 * LM[k, x])][:n]; w = rng.permutation(w[np.argsort(rng.random(len(w)) - 2.0 * RM[k, w])][:n])
        keep = LM[k, x] | RM[k, w] | (rng.random(n) >= drop); x, w = x[keep], w[keep]
        LT[k, x] = w; RT[k, w] = x
    k1 = rng.permutation(E) if order == 0 else np.arange(E); k2 = rng.permutation(E)
    return np.where(LT < 0, W, LT), np.where(RT < 0, W, RT), np.stack([u[k1], np.concatenate([u1, u2])[k2]]), np.stack([v[k1], np.concatenate([y, v2])[k2]])
def make(rng, pick):
    lt = np.zeros((N, 128, W), np.int32); rt = np.zeros((N, 128, W), np.int32); eu = np.zeros((N, 8, 2, E), np.int64); ev = np.zeros((N, 8, 2, E), np.int64)
    for q in range(N):
        for g in range(8):
            s = slice(16 * g, 16 * g + 16)
            lt[q, s], rt[(q + 1) % N, s], eu[q, g], ev[q, g] = graph(rng, *pick(q, g))
    return {"lt": lt, "rt": rt, "eu": np.stack([gtable(x.reshape(8, -1)) for x in eu]), "ev": np.stack([gtable(x.reshape(8, -1)) for x in ev])}
def setup_inputs(rng):
    return make(rng, lambda q, g: (E // 8, int(rng.integers(6, 11)), 0, 0.3 * rng.random(), 0))
def setup_inputs_again(rng):
    return make(rng, lambda q, g: (E // 4, int(rng.integers(6, 11)), 3, 0.3 * rng.random(), 0))
def setup_inputs_long(rng):
    return make(rng, lambda q, g: (0 if (q + g) % 4 == 3 else E // 8, int(rng.integers(6, 11)), 4 if (q + g) % 4 == 3 else 1, 0.3 * rng.random(), 0))
def setup_inputs_order(rng):
    return make(rng, lambda q, g: (E // 8, int(rng.integers(6, 11)), 0, 1.0 if g % 4 < 2 else 0.5, 1 + g % 2))
def setup_inputs_short(rng):
    return make(rng, lambda q, g: (E // 8, int(rng.integers(6, 11)), 2, 0.3 * rng.random(), 0))
def setup_inputs_spread(rng):
    return make(rng, lambda q, g: (int(rng.choice(np.array([1, E // 8]))), int(rng.integers(4, 13)), int(rng.integers(0, 4)), rng.random(), 0))
def load_all(lt, rt, eu, ev):
    none = np.full((8 * N, 16, 1), W, np.int64)
    L = np.concatenate([lt.astype(np.int64).reshape(8 * N, 16, W), none], axis=2)
    R = np.concatenate([np.roll(rt, -1, axis=0).astype(np.int64).reshape(8 * N, 16, W), none], axis=2)
    U, V = [np.stack([gentries(x) for x in t]).astype(np.int64).reshape(8 * N, 2, E) for t in (eu, ev)]
    return L, R, U, V
def turn(L, R, u, v):
    k = np.arange(8 * N)[:, None]
    fu = L[k, :, u] == W; fv = R[k, :, v] == W
    a = np.argmax(fu, axis=2); b = np.argmax(fv, axis=2); free = bool(np.all(np.any(fu, axis=2)) and np.all(np.any(fv, axis=2)))
    xs = [v]
    for i in range(P + 1):
        T = R if i % 2 == 0 else L; x = xs[-1]
        p, q = T[k, a, x], T[k, b, x]
        xs.append(p if i % 2 == 0 else q)
        T[k, a, x] = q; T[k, b, x] = p
    L[k, a, u] = v; R[k, a, v] = u
    return a, free, xs
def check_inputs(d):
    bad = []
    for k, hi in (("lt", W), ("rt", W), ("eu", W - 1), ("ev", W - 1)):
        if np.min(d[k]) < 0 or np.max(d[k]) > hi: bad.append("range of " + k)
    if bad: return bad
    L, R, U, V = load_all(d["lt"], d["rt"], d["eu"], d["ev"]); own = np.arange(W + 1)
    for A, B in ((L, R), (R, L)):
        if np.any((A < W) & (np.take_along_axis(B, A, 2) != own)): bad.append("lt and rt tell the same edges")
    if bad: return bad
    for t in range(2):
        a, free, xs = turn(L, R, U[:, t], V[:, t])
        if not free: bad.append("a free colour at both ends")
        if np.any(xs[P + 1] < W): bad.append("paths of at most P edges")
        for side in ([U[:, t]] + xs[1:P + 1:2], xs[0:P + 1:2]):
            s = np.sort(np.concatenate(side, axis=1), axis=1)
            if np.any((s[:, 1:] == s[:, :-1]) & (s[:, 1:] < W)): bad.append("different vertices in a round")
        if bad: return bad
    return bad
def reference(lt, rt, eu, ev):
    L, R, U, V = load_all(lt, rt, eu, ev); got = []
    for t in range(2):
        a, free, xs = turn(L, R, U[:, t], V[:, t]); got.append(a)
    return {"yl": np.ascontiguousarray(L[:, :, :W]).reshape(N, 128, W).astype(np.float32), "ya": np.concatenate(got, axis=1).reshape(N, 8, 2 * E).astype(np.float32)}

@@ -1,0 +1,517 @@
+from concourse.mybir import AluOpType, ActivationFunctionType
+
+W, E = 2560, 896
+HALF = W // 2
+WG, WS = W + 8, W + E + 8
+SG = 2.0 ** -17
+RCH = [(0, 512), (512, 1536), (1536, 2560)]
+LCH = [(0, 1024), (1024, 2048), (2048, 2560)]
+HV = [(0, 512), (512, 896)]
+
+
+def _sb(cols, dtype):
+    return ("sbuf", [128, cols], dtype)
+
+
+SCRATCH = {
+    "rti": _sb(W, "int32"), "lti": _sb(W, "int32"), "eui": _sb(112, "int32"), "evi": _sb(112, "int32"),
+    "r16": _sb(W, "float16"), "rl16": _sb(W, "float16"),
+    "Lc": _sb(WS, "float32"), "R0": _sb(WG, "float32"), "R1": _sb(WS, "float32"), "DL": _sb(WS, "float32"),
+    "Yo": _sb(W, "float32"), "yas": _sb(2 * E, "float32"),
+    "eu16": _sb(112, "uint16"), "ev16": _sb(112, "uint16"),
+    "wv": _sb(168, "float16"), "X": _sb(3 * E, "float16"), "Pu": _sb(E, "float16"),
+    "qi": _sb(1, "int32"), "si": _sb(1, "int32"), "qf": _sb(1, "float32"), "sf": _sb(1, "float32"),
+    "g16": _sb(1, "float32"), "s14": _sb(1, "float32"), "bB": _sb(1, "float32"),
+    "TT": _sb(144, "float32"), "GP": _sb(128, "float32"), "PS16": _sb(128, "float32"), "Jb": _sb(56, "float32"),
+    "sel": _sb(16, "float32"), "tl": _sb(128, "float32"), "Low": _sb(128, "float32"),
+    "E1": _sb(144, "float16"), "E8": _sb(144, "float16"), "BD1": _sb(128, "float16"), "BDm1": _sb(128, "float16"),
+    "BDp": _sb(128, "float16"), "BDn": _sb(128, "float16"), "I14": _sb(128, "float16"), "Jf": _sb(56, "float16"),
+    "Ib2": _sb(128, "bfloat16"), "Ibm1": _sb(128, "bfloat16"), "Wd5": _sb(128, "bfloat16"), "cBD": _sb(128, "bfloat16"),
+    "ncI": _sb(128, "bfloat16"), "Pfn": _sb(128, "bfloat16"), "Cw": _sb(8, "bfloat16"),
+    "Fu": _sb(E, "bfloat16"), "Fv": _sb(E, "bfloat16"),
+    "tB": _sb(56, "float32"), "mx": _sb(56, "float32"),
+    "PSM": ("psum", [128, 4096], "float32"),
+}
+for _t in range(2):
+    SCRATCH["mA%d" % _t] = _sb(E, "bfloat16")
+    SCRATCH["mB%d" % _t] = _sb(E, "bfloat16")
+    SCRATCH["S%d" % _t] = _sb(E, "float32")
+    SCRATCH["P%d" % _t] = _sb(E, "float32")
+for _i in range(5):
+    SCRATCH["G%d" % _i] = _sb(E, "float16")
+for _i in range(7):
+    SCRATCH["col%d" % _i] = _sb(E, "float32")
+for _i in range(6):
+    SCRATCH["upd%d" % _i] = _sb(E, "float32")
+for _i in range(1, 6):
+    SCRATCH["og%d" % _i] = _sb(56, "uint16")
+    SCRATCH["os%d" % _i] = _sb(56, "uint16")
+
+QSEM = {"g": "cg", "v": "cv", "a": "ca", "p": "cp"}
+DMAS = (["eu", "ev", "r1a", "r1b", "ya0", "ya1"] + ["rt%d" % c for c in range(len(RCH))] + ["lt%d" % c for c in range(len(LCH))]
+        + ["y%d" % b for b in range(5)])
+SEMAPHORES = list(QSEM.values()) + ["d_" + n for n in DMAS] + ["arr%d" % c for c in range(len(RCH))] + ["sent"]
+
+PA, PB, PW1, PW0, PC = 0, 1024, 2048, 2560, 3072
+
+
+def bank(col):
+    return "B%d" % (col // 512)
+
+
+def emit(ops, queues, T):
+    last_w, readers, known, waits, marked = {}, {}, {}, [], set()
+    for n, o in enumerate(ops):
+        deps = set()
+        for k in o["r"]:
+            if k in last_w:
+                deps.add(last_w[k])
+            if k[0] == "B" and len(k) == 2:
+                deps.update(m for m in readers.get(k, []) if ops[m]["q"] != o["q"])
+        for k in o["w"]:
+            if k in last_w:
+                deps.add(last_w[k])
+            deps.update(readers.get(k, []))
+        best = {}
+        for m in deps:
+            p = ops[m]
+            if p["q"] == "p" and o["q"] == "p":
+                continue
+            src = p["sem"] if p["sem"] else p["q"]
+            best[src] = max(best.get(src, -1), m)
+        mine = []
+        if o["q"] is not None:
+            for src in sorted(best):
+                m = best[src]
+                if known.get((o["q"], src), -1) < m:
+                    known[(o["q"], src)] = m
+                    mine.append(m)
+                    marked.add(m)
+        waits.append(mine)
+        for k in o["r"]:
+            readers.setdefault(k, []).append(n)
+        for k in o["w"]:
+            last_w[k] = n
+            readers[k] = []
+    count, value = {}, {}
+    for n, o in enumerate(ops):
+        if o["sem"]:
+            value[n] = (o["sem"], o["n"])
+        elif n in marked:
+            count[o["q"]] = count.get(o["q"], 0) + 1
+            value[n] = (QSEM[o["q"]], count[o["q"]])
+    for n, o in enumerate(ops):
+        if o["q"] is None:
+            continue
+        q = queues[o["q"]]
+        for m in waits[n]:
+            q.wait_ge(T.sem[value[m][0]], value[m][1])
+        if o["f"] is None:
+            continue
+        ins = o["f"]()
+        if o["sem"]:
+            ins.then_inc(T.sem[o["sem"]], o["n"])
+        elif n in marked:
+            ins.then_inc(T.sem[value[n][0]], 1)
+
+
+def rank_program(g, core, T, topo):
+    rank = T.rank_of(core)
+    if rank is None:
+        return
+    A, F = AluOpType, ActivationFunctionType
+    V, SC, PE = g.vector, g.scalar, g.tensor
+    N = len(T.cores)
+    dst = T.cores[(rank - 1) % N]
+    src = T.cores[(rank + 1) % N]
+    rid, pid = topo.addr(dst)[0], topo.addr(dst)[1]
+    n_out, n_in = len(topo.engines(core, dst)), len(topo.engines(src, core))
+    PSM = T.PSM
+    ops = []
+
+    def op(q, f, r, w, sem=None, n=0):
+        ops.append({"q": q, "f": f, "r": list(r), "w": list(w), "sem": sem, "n": n})
+
+    def dma(q, name, out, in_, r, w):
+        eng = {"s": g.sync, "a": g.scalar}[q]
+        op(q, lambda: eng.dma_start(out, in_), r, w, "d_" + name, 16)
+
+    def ts(out, in0, s1, s2, o0, o1, r, w):
+        if s2 is None:
+            op("v", lambda: V.tensor_scalar(out, in0, s1, None, o0), r, w)
+        else:
+            op("v", lambda: V.tensor_scalar(out, in0, s1, s2, o0, o1), r, w)
+
+    def tt(out, in0, in1, o, r, w):
+        op("v", lambda: V.tensor_tensor(out, in0, in1, o), r, w)
+
+    def act(out, in_, func, r, w, bias=None, scale=None):
+        kw = {}
+        if bias is not None:
+            kw["bias"] = bias
+        if scale is not None:
+            kw["scale"] = scale
+        op("a", lambda: SC.activation(out, in_, func, **kw), r, w)
+
+    def mm(out, col, terms):
+        for i, (lh, lk, rh, rk) in enumerate(terms):
+            st, sp = i == 0, i == len(terms) - 1
+            op("p", lambda lh=lh, rh=rh, st=st, sp=sp: PE.matmul(out, lh, rh, st, sp), [lk] + list(rk), [bank(col)])
+
+    def hk(name, hs=(0, 1)):
+        return [name + "." + str(h) for h in hs]
+
+    def both(col):
+        return [bank(col), bank(col + 512)]
+
+    def spread(col, terms, hs=(0, 1), rows=128):
+        for h in hs:
+            a, b = HV[h]
+            mm(PSM[0:rows, col + a:col + b], col + a,
+               [(T[wn][:], wn, T[bn][:, c0 + a:c0 + b], XK if bn == "X" else hk(bn, (h,))) for wn, bn, c0 in terms])
+
+    def offs(name, t, hs):
+        c0 = 56 * t if name in ("eu16", "ev16") else 0
+        return T[name][:, c0 + HV[hs[0]][0] // 16:c0 + HV[hs[-1]][1] // 16]
+
+    def lanes(name, hs):
+        return T[name][:, HV[hs[0]][0]:HV[hs[-1]][1]]
+
+    RK = ["R0.%d" % b for b in range(6)]
+    R1K = ["R1.a", "R1.b", "R1.n"]
+    LK = ["Lc.%d" % c for c in range(len(LCH))] + ["Lc.n"]
+    XK = ["X%d" % s for s in range(16)]
+
+    def rtab(t):
+        return (T.R0, RK) if t == 0 else (T.R1, R1K)
+
+    dma("a", "ev", T.evi[:], T.ev[:], [], ["evi"])
+    dma("a", "eu", T.eui[:], T.eu[:], [], ["eui"])
+    for c, (a, b) in enumerate(RCH):
+        dma("s", "rt%d" % c, T.rti[:, a:b], T.rt[:, a:b], [], ["rti.%d" % c])
+    for c, (a, b) in enumerate(LCH):
+        dma("s", "lt%d" % c, T.lti[:, a:b], T.lt[:, a:b], [], ["lti.%d" % c])
+
+    def iota(name, out, pattern, base, cm, flag=True):
+        if flag:
+            op("g", lambda: g.iota(out, pattern, base, cm, allow_small_or_imprecise_dtypes=True), [], [name])
+        else:
+            op("g", lambda: g.iota(out, pattern, base, cm), [], [name])
+
+    iota("qi", T.qi[:], [[0, 1]], 0, 1, False)
+    iota("qf", T.qf[:], [[0, 1]], 0, 1)
+    iota("GP", T.GP[:], [[16, 8], [0, 16]], 0, 0)
+    iota("TT", T.TT[:], [[1, 144]], -15, 0)
+    iota("PS16", T.PS16[:], [[0, 8], [1, 16]], 0, 0)
+    iota("Jb", T.Jb[:], [[16, 56]], 1, 0)
+    for c in range(len(RCH)):
+        op(None, None, [], ["rl16.%d" % c], "arr%d" % c, n_in)
+
+    op("v", lambda: V.memset(T.Lc[:, W:WG], float(HALF)), [], ["Lc.n"])
+    op("v", lambda: V.memset(T.R0[:, W:WG], HALF * SG), [], ["R0.5"])
+    op("v", lambda: V.memset(T.R1[:, W:WG], HALF * SG), [], ["R1.n"])
+    ts(T.si[:], T.qi[:], 15, None, A.bitwise_and, None, ["qi"], ["si"])
+    ts(T.I14[:], T.TT[:, 15:143], T.qf[:], 2.0 ** -14, A.is_equal, A.mult, ["TT", "qf"], ["I14"])
+    op("v", lambda: V.tensor_copy(T.sf[:], T.si[:]), ["si"], ["sf"])
+    ts(T.Ibm1[:], T.TT[:, 15:143], T.qf[:], -1.0, A.is_equal, A.mult, ["TT", "qf"], ["Ibm1"])
+    tt(T.g16[:], T.qf[:], T.sf[:], A.subtract, ["qf", "sf"], ["g16"])
+    ts(T.s14[:], T.sf[:], 2.0 ** -14, None, A.mult, None, ["sf"], ["s14"])
+    ts(T.bB[:], T.sf[:], -0.5, 0.5, A.mult, A.add, ["sf"], ["bB"])
+    ts(T.sel[:], T.PS16[:, 0:16], T.sf[:], None, A.is_equal, None, ["PS16", "sf"], ["sel"])
+    ts(T.tl[:], T.PS16[:], T.sf[:], None, A.is_gt, None, ["PS16", "sf"], ["tl"])
+    for name, val in (("BD1", 1.0), ("Wd5", float(HALF)), ("BDm1", -1.0), ("BDp", 2.0 ** -14), ("BDn", -2.0 ** -14)):
+        ts(T[name][:], T.GP[:], T.g16[:], val, A.is_equal, A.mult, ["GP", "g16"], [name])
+    tt(T.Low[:], T.tl[:], T.BD1[:], A.mult, ["tl", "BD1"], ["Low"])
+    for name, val in (("E1", 1.0), ("E8", 8.0)):
+        ts(T[name][:], T.TT[:], T.g16[:], val, A.is_equal, A.mult, ["TT", "g16"], [name])
+    tt(T.Pfn[:], T.Low[:], T.Ibm1[:], A.add, ["Low", "Ibm1"], ["Pfn"])
+    ts(T.Cw[:], T.GP[:, 0:128:16], T.g16[:], T.s14[:], A.is_equal, A.mult, ["GP", "g16", "s14"], ["Cw"])
+    ts(T.Jf[:], T.Jb[:], T.sf[:], 2.0, A.add, A.mult, ["Jb", "sf"], ["Jf"])
+    act(T.Ib2[:], T.Ibm1[:], F.Copy, ["Ibm1"], ["Ib2"], scale=-0.25)
+    act(T.ncI[:], T.Ibm1[:], F.Copy, ["Ibm1"], ["ncI"], scale=HALF * 2.0 ** -31)
+    act(T.cBD[:], T.Wd5[:], F.Copy, ["Wd5"], ["cBD"], scale=2.0 ** -31)
+
+    def send(c):
+        a, b = RCH[c]
+        ts(T.r16[:, a:b], T.rti[:, a:b], -float(HALF), None, A.add, None, ["rti.%d" % c], ["r16.%d" % c])
+        op("g", lambda: g.remote_dma(T.rl16[:, a:b], T.r16[:, a:b], T.sem["arr%d" % c], T.sem.sent, pid, rid,
+                                     topo.mask(core, dst)), ["r16.%d" % c], [])
+
+    send(0)
+    op("v", lambda: V.tensor_copy(T.ev16[:], T.evi[:]), ["evi"], ["ev16"])
+    op("v", lambda: V.tensor_copy(T.eu16[:], T.eui[:]), ["eui"], ["eu16"])
+    ts(T.wv[:, 0:112], T.evi[:], -float(HALF), -1.0, A.add, A.mult, ["evi"], ["wv.0"])
+    ts(T.wv[:, 112:168], T.eui[:, 0:56], -float(HALF), 0.125, A.add, A.mult, ["eui"], ["wv.1"])
+    send(1)
+
+    def xpart(s0, s1):
+        for s in range(s0, s1):
+            ts(T.X[:, s:3 * E:16], T.wv[:], T.sel[:, s:s + 1], None, A.mult, None, ["wv.0", "wv.1", "sel"], ["X%d" % s])
+
+    xpart(0, 6)
+    send(2)
+    xpart(6, 16)
+    iota("DL", T.DL[:, 0:W], [[0, W]], 0, 0)
+    for c, (a, b) in enumerate(LCH):
+        ts(T.Lc[:, a:b], T.lti[:, a:b], -float(HALF), None, A.add, None, ["lti.%d" % c], ["Lc.%d" % c])
+
+    def rconv(b, on_vector=False):
+        c = [i for i, (x, y) in enumerate(RCH) if x <= 512 * b < y][0]
+        sl = slice(512 * b, 512 * b + 512)
+        if on_vector:
+            ts(T.R0[:, sl], T.rl16[:, sl], SG, None, A.mult, None, ["rl16.%d" % c], ["R0.%d" % b])
+        else:
+            col = PA + 512 * (b % 2)
+            mm(PSM[:, col:col + 512], col, [(T.I14[:], "I14", T.rl16[:, sl], ["rl16.%d" % c])])
+            act(T.R0[:, sl], PSM[:, col:col + 512], F.Copy, [bank(col)], ["R0.%d" % b], scale=0.125)
+
+    def prefix(fb, col, h):
+        spread(col, [("Pfn", fb, 0)], (h,))
+
+    def mask_a(t, col, h):
+        a, b = HV[h]
+        act(lanes("mA%d" % t, (h,)), PSM[:, col + a:col + b], F.Relu, [bank(col + a)], hk("mA%d" % t, (h,)), scale=-16384.0)
+
+    def mask_b(t, col, h):
+        a, b = HV[h]
+        act(lanes("mB%d" % t, (h,)), PSM[:, col + a:col + b], F.Relu, [bank(col + a), "bB"], hk("mB%d" % t, (h,)),
+            bias=T.bB[:], scale=-0.5)
+
+    def free_u(t, h):
+        ts(lanes("Fu", (h,)), T.Lc[:, 0:WG].indirect(offs("eu16", t, (h,))), HALF - 0.5, None, A.is_ge, None,
+           LK + ["eu16"], hk("Fu", (h,)))
+
+    def free_v(t, h):
+        tab, keys = rtab(t)
+        act(lanes("Fv", (h,)), tab[:, 0:WG].indirect(offs("ev16", t, (h,))), F.Sign, keys + ["ev16"], hk("Fv", (h,)),
+            bias=0.5 - HALF, scale=1.0 / SG)
+
+    def make_p(t, col):
+        spread(col, [("BD1", "X", t * E), ("Ib2", "mA%d" % t, 0)])
+        act(T["P%d" % t][:], PSM[:, col:col + E], F.Relu, both(col), hk("P%d" % t), bias=float(HALF - 4096))
+
+    def make_s(t, col):
+        spread(col, [("Ib2", "mA%d" % t, 0), ("Ibm1", "mB%d" % t, 0)])
+        act(T["S%d" % t][:], PSM[:, col:col + E], F.Sign, both(col), hk("S%d" % t))
+
+    def colours(t, col):
+        spread(col, [("Cw", "mA%d" % t, 0)], rows=8)
+        act(T.yas[0:8, t * E:(t + 1) * E], PSM[0:8, col:col + E], F.Copy, both(col), ["yas%d" % t])
+        dma("s", "ya%d" % t, T.ya[:, t * E:(t + 1) * E], T.yas[0:8, t * E:(t + 1) * E], ["yas%d" % t], ["out.ya%d" % t])
+
+    def gather_col(i, t=0):
+        on = "eu16" if i == 6 else ("ev16" if i == 0 else "og%d" % i)
+        tab, keys = rtab(t) if i in (0, 2, 4) else (T.Lc, LK)
+        act(T["col%d" % i][:], tab[:, 0:WG].indirect(offs(on, t, (0, 1))), F.Copy, keys + [on], hk("col%d" % i))
+
+    def wcol(t, i):
+        return PW1 if t == 0 and i % 2 else PW0
+
+    def walk(t, i, hs=(0, 1)):
+        on = "ev16" if i == 0 else "og%d" % i
+        tab, keys = rtab(t) if i % 2 == 0 else (T.Lc, LK)
+        mk = ("mA%d" if i % 2 == 0 else "mB%d") % t
+        tt(lanes("G%d" % i, hs), tab[:, 0:WG].indirect(offs(on, t, hs)), lanes(mk, hs), A.mult,
+           keys + [on] + hk(mk, hs), hk("G%d" % i, hs))
+
+    def wrap(t, i):
+        col = wcol(t, i)
+        en = "E8" if i % 2 == 0 else "E1"
+        terms = [(T.I14[:], "I14", T.Jf[:], ["Jf"])]
+        terms += [(T[en][:, 15 - s:143 - s], en, T["G%d" % i][:, s:E:16], hk("G%d" % i)) for s in range(16)]
+        mm(PSM[:, col:col + 56], col, terms)
+
+    def off_g(t, i):
+        col = wcol(t, i - 1)
+        ts(T["og%d" % i][:], PSM[:, col:col + 56], HALF + 0.2, None, A.add, None, [bank(col)], ["og%d" % i])
+
+    def off_s(t, i, part):
+        col = wcol(t, i - 1)
+        if part == 0:
+            ts(T.tB[:], PSM[:, col:col + 56], HALF / 8192.0 - HALF, 8192.0, A.add, A.mult, [bank(col)], ["tB"])
+        elif part == 1:
+            tt(T.mx[:], PSM[:, col:col + 56], T.tB[:], A.max, [bank(col), "tB"], ["mx"])
+        else:
+            ts(T["os%d" % i][:], T.mx[:], HALF + 0.2, None, A.add, None, ["mx"], ["os%d" % i])
+
+    def diff(t, i, col):
+        if i == 0:
+            terms = [("cBD", "mA0", 0), ("ncI", "mA0", 0), ("I14", "Pu", 0), ("BDn", "G0", 0)]
+        elif i == 1:
+            terms = [("BD1", "X", t * E), ("BD1", "G1", 0)]
+        elif i == 5:
+            terms = [("Wd5", "mB%d" % t, 0), ("BDm1", "G3", 0)]
+        elif i == 3:
+            terms = [("BDm1", "G1", 0), ("BD1", "G3", 0)]
+        else:
+            terms = [("BDp", "G%d" % (i - 2), 0), ("BDn", "G%d" % i, 0)]
+        spread(col, terms)
+
+    def times_s(i, col):
+        if i % 2 == 0:
+            tt(PSM[:, col:col + E], PSM[:, col:col + E], T.S0[:], A.mult, both(col) + hk("S0"), both(col))
+        else:
+            tt(T["upd%d" % i][:], PSM[:, col:col + E], T.S0[:], A.mult, both(col) + hk("S0"), hk("upd%d" % i))
+
+    def add_col(i, col):
+        tt(T["upd%d" % i][:], PSM[:, col:col + E], T["col%d" % i][:], A.add, both(col) + hk("col%d" % i), hk("upd%d" % i))
+
+    def scat_r(i):
+        on = "ev16" if i == 0 else "os%d" % i
+        act(T.R1[:, 0:WS].indirect(offs(on, 0, (0, 1))), T["upd%d" % i][:], F.Tanh, [on] + hk("upd%d" % i), R1K)
+
+    def scat_l(i):
+        tt(T.Lc[:, 0:WS].indirect(offs("os%d" % i, 0, (0, 1))), T["col%d" % i][:], T["upd%d" % i][:], A.add,
+           ["os%d" % i] + hk("col%d" % i) + hk("upd%d" % i), LK)
+
+    rconv(0)
+    rconv(1)
+    rconv(2)
+    dma("s", "r1a", T.R1[:, 0:1536], T.R0[:, 0:1536], RK[0:3], ["R1.a"])
+    spread(PC, [("BDp", "X", 2 * E)])
+    free_u(0, 0)
+    free_u(0, 1)
+    gather_col(6)
+    for h in (0, 1):
+        prefix("Fu", PB, h)
+        mask_a(0, PB, h)
+    rconv(3, True)
+    rconv(4, True)
+    dma("s", "r1b", T.R1[:, 1536:W], T.R0[:, 1536:W], RK[3:5], ["R1.b"])
+    make_p(0, PA)
+    free_v(0, 0)
+    free_v(0, 1)
+    walk(0, 0)
+    wrap(0, 0)
+    for h in (0, 1):
+        prefix("Fv", PB, h)
+        mask_b(0, PB, h)
+    tt(T.Pu[:], PSM[:, PC:PC + E], T.mA0[:], A.mult, both(PC) + hk("mA0"), hk("Pu"))
+    off_g(0, 1)
+    off_s(0, 1, 0)
+    tt(T.Lc[:, 0:WS].indirect(offs("eu16", 0, (0, 1))), T.col6[:], T.P0[:], A.subtract, ["eu16"] + hk("col6") + hk("P0"), LK)
+    make_s(0, PA)
+    gather_col(0)
+    diff(0, 0, PB)
+    gather_col(1)
+    off_s(0, 1, 1)
+    walk(0, 1)
+    wrap(0, 1)
+    diff(0, 1, PC)
+    off_s(0, 1, 2)
+    times_s(0, PB)
+    add_col(0, PB)
+    off_g(0, 2)
+    off_s(0, 2, 0)
+    gather_col(2)
+    scat_r(0)
+    walk(0, 2)
+    wrap(0, 2)
+    diff(0, 2, PA)
+    off_s(0, 2, 1)
+    times_s(1, PC)
+    off_s(0, 2, 2)
+    scat_l(1)
+    off_g(0, 3)
+    off_s(0, 3, 0)
+    gather_col(3)
+    walk(0, 3)
+    wrap(0, 3)
+    diff(0, 3, PB)
+    colours(0, PC)
+    off_s(0, 3, 1)
+    times_s(2, PA)
+    off_s(0, 3, 2)
+    add_col(2, PA)
+    off_g(0, 4)
+    off_s(0, 4, 0)
+    gather_col(4)
+    diff(0, 5, PA)
+    walk(0, 4)
+    wrap(0, 4)
+    diff(0, 4, PC)
+    off_s(0, 4, 1)
+    times_s(3, PB)
+    off_s(0, 4, 2)
+    off_g(0, 5)
+    off_s(0, 5, 0)
+    gather_col(5)
+    scat_r(2)
+    times_s(5, PA)
+    off_s(0, 5, 1)
+    times_s(4, PC)
+    off_s(0, 5, 2)
+    add_col(4, PC)
+    scat_r(4)
+    scat_l(3)
+    free_v(1, 0)
+    free_v(1, 1)
+    for h in (0, 1):
+        prefix("Fv", PC, h)
+        mask_b(1, PC, h)
+    scat_l(5)
+
+    def scat_d(i, hs):
+        if i == 6:
+            ts(T.DL[:, 0:WS].indirect(offs("eu16", 1, hs)), lanes("P1", hs), -1.0, 0.0, A.mult, A.add,
+               ["eu16"] + hk("P1", hs), ["DL"])
+        else:
+            tt(T.DL[:, 0:WS].indirect(offs("os%d" % i, 1, hs)), lanes("upd%d" % i, hs), lanes("S1", hs), A.mult,
+               ["os%d" % i] + hk("upd%d" % i, hs) + hk("S1", hs), ["DL"])
+
+    def diff_out(i):
+        diff(1, i, PC)
+        act(T["upd%d" % i][:], PSM[:, PC:PC + E], F.Copy, both(PC), hk("upd%d" % i))
+
+    free_u(1, 0)
+    free_u(1, 1)
+    for h in (0, 1):
+        prefix("Fu", PB, h)
+        mask_a(1, PB, h)
+    walk(1, 0, (0,))
+    walk(1, 0, (1,))
+    make_p(1, PA)
+    wrap(1, 0)
+    make_s(1, PB)
+    scat_d(6, (0,))
+    off_g(1, 1)
+    off_s(1, 1, 0)
+    walk(1, 1)
+    off_s(1, 1, 1)
+    wrap(1, 1)
+    diff_out(1)
+    colours(1, PB)
+    for b in range(5):
+        act(PSM[:, 512 * b:512 * b + 512], T.Lc[:, 512 * b:512 * b + 512], F.Identity, LK, [bank(512 * b)], bias=float(HALF))
+    scat_d(6, (1,))
+    off_s(1, 1, 2)
+    off_g(1, 2)
+    walk(1, 2)
+    wrap(1, 2)
+    scat_d(1, (0,))
+    off_g(1, 3)
+    off_s(1, 3, 0)
+    walk(1, 3)
+    off_s(1, 3, 1)
+    wrap(1, 3)
+    diff_out(3)
+    scat_d(1, (1,))
+    off_s(1, 3, 2)
+    off_g(1, 4)
+    walk(1, 4)
+    wrap(1, 4)
+    diff_out(5)
+    scat_d(3, (0,))
+    off_s(1, 5, 0)
+    scat_d(3, (1,))
+    off_s(1, 5, 1)
+    off_s(1, 5, 2)
+    scat_d(5, (0, 1))
+    for b in range(5):
+        sl = slice(512 * b, 512 * b + 512)
+        tt(T.Yo[:, sl], PSM[:, sl], T.DL[:, sl], A.add, [bank(512 * b), "DL"], ["Yo%d" % b])
+        dma("s" if b % 2 == 0 else "a", "y%d" % b, T.yl[:, sl], T.Yo[:, sl], ["Yo%d" % b], ["out.y%d" % b])
+    op("s", None, ["out.y%d" % b for b in range(5)] + ["out.ya0", "out.ya1"], [])
+
+    emit(ops, {"g": g, "v": V, "a": SC, "p": PE, "s": g.sync}, T)
+    g.wait_ge(T.sem.sent, n_out * len(RCH))

@@ -4,55 +4,30 @@ W, E = 2560, 896
 HALF = W // 2
 WG, WS = W + 8, W + E + 8
 SG = 2.0 ** -17
-RCH = [(0, 512), (512, 1536), (1536, 2560)]
+RCH = [(0, 256), (256, 1024), (1024, 1792), (1792, 2560)]
+RP = [(0, 256, 0), (256, 640, 1), (640, 1024, 1), (1024, 1408, 2), (1408, 1792, 2), (1792, 2176, 3), (2176, 2560, 3)]
 LCH = [(0, 1024), (1024, 2048), (2048, 2560)]
 HV = [(0, 512), (512, 896)]
-
-
-def _sb(cols, dtype):
-    return ("sbuf", [128, cols], dtype)
-
-
-SCRATCH = {
-    "rti": _sb(W, "int32"), "lti": _sb(W, "int32"), "eui": _sb(112, "int32"), "evi": _sb(112, "int32"),
-    "r16": _sb(W, "float16"), "rl16": _sb(W, "float16"),
-    "Lc": _sb(WS, "float32"), "R0": _sb(WG, "float32"), "R1": _sb(WS, "float32"), "DL": _sb(WS, "float32"),
-    "Yo": _sb(W, "float32"), "yas": _sb(2 * E, "float32"),
-    "eu16": _sb(112, "uint16"), "ev16": _sb(112, "uint16"),
-    "wv": _sb(168, "float16"), "X": _sb(3 * E, "float16"), "Pu": _sb(E, "float16"),
-    "qi": _sb(1, "int32"), "si": _sb(1, "int32"), "qf": _sb(1, "float32"), "sf": _sb(1, "float32"),
-    "g16": _sb(1, "float32"), "s14": _sb(1, "float32"), "bB": _sb(1, "float32"),
-    "TT": _sb(144, "float32"), "GP": _sb(128, "float32"), "PS16": _sb(128, "float32"), "Jb": _sb(56, "float32"),
-    "sel": _sb(16, "float32"), "tl": _sb(128, "float32"), "Low": _sb(128, "float32"),
-    "E1": _sb(144, "float16"), "E8": _sb(144, "float16"), "BD1": _sb(128, "float16"), "BDm1": _sb(128, "float16"),
-    "BDp": _sb(128, "float16"), "BDn": _sb(128, "float16"), "I14": _sb(128, "float16"), "Jf": _sb(56, "float16"),
-    "Ib2": _sb(128, "bfloat16"), "Ibm1": _sb(128, "bfloat16"), "Wd5": _sb(128, "bfloat16"), "cBD": _sb(128, "bfloat16"),
-    "ncI": _sb(128, "bfloat16"), "Pfn": _sb(128, "bfloat16"), "Cw": _sb(8, "bfloat16"),
-    "Fu": _sb(E, "bfloat16"), "Fv": _sb(E, "bfloat16"),
-    "tB": _sb(56, "float32"), "mx": _sb(56, "float32"),
-    "PSM": ("psum", [128, 4096], "float32"),
-}
-for _t in range(2):
-    SCRATCH["mA%d" % _t] = _sb(E, "bfloat16")
-    SCRATCH["mB%d" % _t] = _sb(E, "bfloat16")
-    SCRATCH["S%d" % _t] = _sb(E, "float32")
-    SCRATCH["P%d" % _t] = _sb(E, "float32")
-for _i in range(5):
-    SCRATCH["G%d" % _i] = _sb(E, "float16")
-for _i in range(7):
-    SCRATCH["col%d" % _i] = _sb(E, "float32")
-for _i in range(6):
-    SCRATCH["upd%d" % _i] = _sb(E, "float32")
-for _i in range(1, 6):
-    SCRATCH["og%d" % _i] = _sb(56, "uint16")
-    SCRATCH["os%d" % _i] = _sb(56, "uint16")
+SCRATCH = {"PSM": ("psum", [128, 4096], "float32")}
+for _d, _l in (
+        ("int32", [("rti", W), ("lti", W), ("eui", 112), ("evi", 112), ("qi", 1), ("si", 1)]),
+        ("uint16", [("eu16", 112), ("ev16", 112), ("osb", 336)] + [("og%d" % i, 56) for i in range(1, 6)]),
+        ("float16", [("r16", W), ("rl16", W), ("wv", 168), ("X", 3 * E), ("Pu", E), ("Jf", 56)] + [("G%d" % i, E) for i in range(5)]),
+        ("bfloat16", [("E1", 144), ("E8", 144), ("Cw", 8)]
+         + [(n, 128) for n in ("BD1", "BDm1", "BDp", "BDn", "I14", "Ib2", "Ibm1", "Wd5", "cBD", "ncI", "Pfn")]
+         + [(n, E) for n in ("Fu", "Fv", "mA0", "mA1", "mB0", "mB1")]),
+        ("float32", [("Lc", WS), ("R0", WG), ("R1", WS), ("DL", WS), ("Yo", W), ("yas", 2 * E), ("TT", 144), ("GP", 128),
+                     ("PS16", 128), ("Jb", 56), ("sel", 16), ("tl", 128), ("Low", 128), ("tB", 112), ("mx", 112)]
+         + [(n, 1) for n in ("qf", "sf", "g16", "s14", "bB")] + [(n, E) for n in ("S0", "S1", "P0", "P1")]
+         + [("col%d" % i, E) for i in range(7)] + [("upd%d" % i, E) for i in range(6)])):
+    for _n, _c in _l:
+        SCRATCH[_n] = ("sbuf", [128, _c], _d)
 
 QSEM = {"g": "cg", "v": "cv", "a": "ca", "p": "cp"}
 DMAS = (["eu", "ev", "r1a", "r1b", "ya0", "ya1"] + ["rt%d" % c for c in range(len(RCH))] + ["lt%d" % c for c in range(len(LCH))]
         + ["y%d" % b for b in range(5)])
 SEMAPHORES = list(QSEM.values()) + ["d_" + n for n in DMAS] + ["arr%d" % c for c in range(len(RCH))] + ["sent"]
-
-PA, PB, PW1, PW0, PC = 0, 1024, 2048, 2560, 3072
+PA, PB, PW0, PC = 0, 1024, 2560, 3072
 
 
 def bank(col):
@@ -153,9 +128,9 @@ def rank_program(g, core, T, topo):
             kw["scale"] = scale
         op("a", lambda: SC.activation(out, in_, func, **kw), r, w)
 
-    def mm(out, col, terms):
+    def mm(out, col, terms, first=True, last=True):
         for i, (lh, lk, rh, rk) in enumerate(terms):
-            st, sp = i == 0, i == len(terms) - 1
+            st, sp = first and i == 0, last and i == len(terms) - 1
             op("p", lambda lh=lh, rh=rh, st=st, sp=sp: PE.matmul(out, lh, rh, st, sp), [lk] + list(rk), [bank(col)])
 
     def hk(name, hs=(0, 1)):
@@ -164,20 +139,22 @@ def rank_program(g, core, T, topo):
     def both(col):
         return [bank(col), bank(col + 512)]
 
-    def spread(col, terms, hs=(0, 1), rows=128):
+    def spread(col, terms, hs=(0, 1), rows=128, first=True, last=True):
         for h in hs:
             a, b = HV[h]
             mm(PSM[0:rows, col + a:col + b], col + a,
-               [(T[wn][:], wn, T[bn][:, c0 + a:c0 + b], XK if bn == "X" else hk(bn, (h,))) for wn, bn, c0 in terms])
+               [(T[wn][:], wn, T[bn][:, c0 + a:c0 + b], XK if bn == "X" else hk(bn, (h,))) for wn, bn, c0 in terms], first, last)
 
     def offs(name, t, hs):
         c0 = 56 * t if name in ("eu16", "ev16") else 0
+        if name[:2] == "os":
+            name, c0 = "osb", 56 * int(name[2])
         return T[name][:, c0 + HV[hs[0]][0] // 16:c0 + HV[hs[-1]][1] // 16]
 
     def lanes(name, hs):
         return T[name][:, HV[hs[0]][0]:HV[hs[-1]][1]]
 
-    RK = ["R0.%d" % b for b in range(6)]
+    RK = ["R0.%d" % b for b in range(len(RP))] + ["R0.n"]
     R1K = ["R1.a", "R1.b", "R1.n"]
     LK = ["Lc.%d" % c for c in range(len(LCH))] + ["Lc.n"]
     XK = ["X%d" % s for s in range(16)]
@@ -200,36 +177,13 @@ def rank_program(g, core, T, topo):
 
     iota("qi", T.qi[:], [[0, 1]], 0, 1, False)
     iota("qf", T.qf[:], [[0, 1]], 0, 1)
-    iota("GP", T.GP[:], [[16, 8], [0, 16]], 0, 0)
     iota("TT", T.TT[:], [[1, 144]], -15, 0)
     iota("PS16", T.PS16[:], [[0, 8], [1, 16]], 0, 0)
+    iota("GP", T.GP[:], [[16, 8], [0, 16]], 0, 0)
     iota("Jb", T.Jb[:], [[16, 56]], 1, 0)
+    iota("Lc.n", T.Lc[:, W:WG], [[0, 8]], HALF, 0)
     for c in range(len(RCH)):
         op(None, None, [], ["rl16.%d" % c], "arr%d" % c, n_in)
-
-    op("v", lambda: V.memset(T.Lc[:, W:WG], float(HALF)), [], ["Lc.n"])
-    op("v", lambda: V.memset(T.R0[:, W:WG], HALF * SG), [], ["R0.5"])
-    op("v", lambda: V.memset(T.R1[:, W:WG], HALF * SG), [], ["R1.n"])
-    ts(T.si[:], T.qi[:], 15, None, A.bitwise_and, None, ["qi"], ["si"])
-    ts(T.I14[:], T.TT[:, 15:143], T.qf[:], 2.0 ** -14, A.is_equal, A.mult, ["TT", "qf"], ["I14"])
-    op("v", lambda: V.tensor_copy(T.sf[:], T.si[:]), ["si"], ["sf"])
-    ts(T.Ibm1[:], T.TT[:, 15:143], T.qf[:], -1.0, A.is_equal, A.mult, ["TT", "qf"], ["Ibm1"])
-    tt(T.g16[:], T.qf[:], T.sf[:], A.subtract, ["qf", "sf"], ["g16"])
-    ts(T.s14[:], T.sf[:], 2.0 ** -14, None, A.mult, None, ["sf"], ["s14"])
-    ts(T.bB[:], T.sf[:], -0.5, 0.5, A.mult, A.add, ["sf"], ["bB"])
-    ts(T.sel[:], T.PS16[:, 0:16], T.sf[:], None, A.is_equal, None, ["PS16", "sf"], ["sel"])
-    ts(T.tl[:], T.PS16[:], T.sf[:], None, A.is_gt, None, ["PS16", "sf"], ["tl"])
-    for name, val in (("BD1", 1.0), ("Wd5", float(HALF)), ("BDm1", -1.0), ("BDp", 2.0 ** -14), ("BDn", -2.0 ** -14)):
-        ts(T[name][:], T.GP[:], T.g16[:], val, A.is_equal, A.mult, ["GP", "g16"], [name])
-    tt(T.Low[:], T.tl[:], T.BD1[:], A.mult, ["tl", "BD1"], ["Low"])
-    for name, val in (("E1", 1.0), ("E8", 8.0)):
-        ts(T[name][:], T.TT[:], T.g16[:], val, A.is_equal, A.mult, ["TT", "g16"], [name])
-    tt(T.Pfn[:], T.Low[:], T.Ibm1[:], A.add, ["Low", "Ibm1"], ["Pfn"])
-    ts(T.Cw[:], T.GP[:, 0:128:16], T.g16[:], T.s14[:], A.is_equal, A.mult, ["GP", "g16", "s14"], ["Cw"])
-    ts(T.Jf[:], T.Jb[:], T.sf[:], 2.0, A.add, A.mult, ["Jb", "sf"], ["Jf"])
-    act(T.Ib2[:], T.Ibm1[:], F.Copy, ["Ibm1"], ["Ib2"], scale=-0.25)
-    act(T.ncI[:], T.Ibm1[:], F.Copy, ["Ibm1"], ["ncI"], scale=HALF * 2.0 ** -31)
-    act(T.cBD[:], T.Wd5[:], F.Copy, ["Wd5"], ["cBD"], scale=2.0 ** -31)
 
     def send(c):
         a, b = RCH[c]
@@ -237,33 +191,56 @@ def rank_program(g, core, T, topo):
         op("g", lambda: g.remote_dma(T.rl16[:, a:b], T.r16[:, a:b], T.sem["arr%d" % c], T.sem.sent, pid, rid,
                                      topo.mask(core, dst)), ["r16.%d" % c], [])
 
+    ts(T.si[:], T.qi[:], 15, None, A.bitwise_and, None, ["qi"], ["si"])
+    op("v", lambda: V.tensor_copy(T.sf[:], T.si[:]), ["si"], ["sf"])
+    tt(T.g16[:], T.qf[:], T.sf[:], A.subtract, ["qf", "sf"], ["g16"])
+    ts(T.Ibm1[:], T.TT[:, 15:143], T.qf[:], -1.0, A.is_equal, A.mult, ["TT", "qf"], ["Ibm1"])
+    ts(T.E1[:], T.TT[:], T.g16[:], None, A.is_equal, None, ["TT", "g16"], ["E1"])
+    act(T.s14[:], T.sf[:], F.Copy, ["sf"], ["s14"], scale=2.0 ** -14)
+    act(T.bB[:], T.sf[:], F.Identity, ["sf"], ["bB"], bias=0.5, scale=-0.5)
+    ts(T.sel[:], T.PS16[:, 0:16], T.sf[:], None, A.is_equal, None, ["PS16", "sf"], ["sel"])
+    ts(T.tl[:], T.PS16[:], T.sf[:], None, A.is_gt, None, ["PS16", "sf"], ["tl"])
+    ts(T.BD1[:], T.GP[:], T.g16[:], None, A.is_equal, None, ["GP", "g16"], ["BD1"])
+    ts(T.Cw[:], T.GP[:, 0:128:16], T.g16[:], T.s14[:], A.is_equal, A.mult, ["GP", "g16", "s14"], ["Cw"])
     send(0)
+    for name, base, val in (("I14", "Ibm1", -2.0 ** -14), ("Ib2", "Ibm1", -0.25), ("ncI", "Ibm1", HALF * 2.0 ** -31),
+                            ("E8", "E1", 8.0), ("Wd5", "BD1", float(HALF)), ("BDm1", "BD1", -1.0), ("BDp", "BD1", 2.0 ** -14),
+                            ("BDn", "BD1", -2.0 ** -14), ("cBD", "BD1", HALF * 2.0 ** -31)):
+        act(T[name][:], T[base][:], F.Copy, [base], [name], scale=val)
+    act(T.R0[:, W:WG], T.Lc[:, W:WG], F.Copy, ["Lc.n"], ["R0.n"], scale=SG)
+    act(T.R1[:, W:WG], T.Lc[:, W:WG], F.Copy, ["Lc.n"], ["R1.n"], scale=SG)
+    tt(T.Low[:], T.tl[:], T.BD1[:], A.mult, ["tl", "BD1"], ["Low"])
+    ts(T.Jf[:], T.Jb[:], T.sf[:], 2.0, A.add, A.mult, ["Jb", "sf"], ["Jf"])
     op("v", lambda: V.tensor_copy(T.ev16[:], T.evi[:]), ["evi"], ["ev16"])
     op("v", lambda: V.tensor_copy(T.eu16[:], T.eui[:]), ["eui"], ["eu16"])
     ts(T.wv[:, 0:112], T.evi[:], -float(HALF), -1.0, A.add, A.mult, ["evi"], ["wv.0"])
     ts(T.wv[:, 112:168], T.eui[:, 0:56], -float(HALF), 0.125, A.add, A.mult, ["eui"], ["wv.1"])
-    send(1)
+    tt(T.Pfn[:], T.Low[:], T.Ibm1[:], A.add, ["Low", "Ibm1"], ["Pfn"])
 
     def xpart(s0, s1):
         for s in range(s0, s1):
             ts(T.X[:, s:3 * E:16], T.wv[:], T.sel[:, s:s + 1], None, A.mult, None, ["wv.0", "wv.1", "sel"], ["X%d" % s])
 
-    xpart(0, 6)
+    send(1)
+    xpart(0, 5)
     send(2)
-    xpart(6, 16)
+    xpart(5, 10)
+    send(3)
+    xpart(10, 13)
     iota("DL", T.DL[:, 0:W], [[0, W]], 0, 0)
     for c, (a, b) in enumerate(LCH):
         ts(T.Lc[:, a:b], T.lti[:, a:b], -float(HALF), None, A.add, None, ["lti.%d" % c], ["Lc.%d" % c])
+    xpart(13, 16)
 
     def rconv(b, on_vector=False):
-        c = [i for i, (x, y) in enumerate(RCH) if x <= 512 * b < y][0]
-        sl = slice(512 * b, 512 * b + 512)
+        x, y, c = RP[b]
+        sl = slice(x, y)
         if on_vector:
             ts(T.R0[:, sl], T.rl16[:, sl], SG, None, A.mult, None, ["rl16.%d" % c], ["R0.%d" % b])
         else:
-            col = PA + 512 * (b % 2)
-            mm(PSM[:, col:col + 512], col, [(T.I14[:], "I14", T.rl16[:, sl], ["rl16.%d" % c])])
-            act(T.R0[:, sl], PSM[:, col:col + 512], F.Copy, [bank(col)], ["R0.%d" % b], scale=0.125)
+            col = (PA if b < 5 else PB) + 512 * (b % 2)
+            mm(PSM[:, col:col + y - x], col, [(T.I14[:], "I14", T.rl16[:, sl], ["rl16.%d" % c])])
+            act(T.R0[:, sl], PSM[:, col:col + y - x], F.Copy, [bank(col)], ["R0.%d" % b], scale=0.125)
 
     def prefix(fb, col, h):
         spread(col, [("Pfn", fb, 0)], (h,))
@@ -287,12 +264,17 @@ def rank_program(g, core, T, topo):
             bias=0.5 - HALF, scale=1.0 / SG)
 
     def make_p(t, col):
-        spread(col, [("BD1", "X", t * E), ("Ib2", "mA%d" % t, 0)])
-        act(T["P%d" % t][:], PSM[:, col:col + E], F.Relu, both(col), hk("P%d" % t), bias=float(HALF - 4096))
+        for h in (0, 1):
+            a, b = HV[h]
+            spread(col, [("BD1", "X", t * E), ("Ib2", "mA%d" % t, 0)], (h,))
+            act(lanes("P%d" % t, (h,)), PSM[:, col + a:col + b], F.Relu, [bank(col + a)], hk("P%d" % t, (h,)),
+                bias=float(HALF - 4096))
 
     def make_s(t, col):
-        spread(col, [("Ib2", "mA%d" % t, 0), ("Ibm1", "mB%d" % t, 0)])
-        act(T["S%d" % t][:], PSM[:, col:col + E], F.Sign, both(col), hk("S%d" % t))
+        for h in (0, 1):
+            a, b = HV[h]
+            spread(col, [("Ib2", "mA%d" % t, 0), ("Ibm1", "mB%d" % t, 0)], (h,))
+            act(lanes("S%d" % t, (h,)), PSM[:, col + a:col + b], F.Sign, [bank(col + a)], hk("S%d" % t, (h,)))
 
     def colours(t, col):
         spread(col, [("Cw", "mA%d" % t, 0)], rows=8)
@@ -305,7 +287,7 @@ def rank_program(g, core, T, topo):
         act(T["col%d" % i][:], tab[:, 0:WG].indirect(offs(on, t, (0, 1))), F.Copy, keys + [on], hk("col%d" % i))
 
     def wcol(t, i):
-        return PW1 if t == 0 and i % 2 else PW0
+        return PW0 - 56 if t == 0 and i % 2 else PW0
 
     def walk(t, i, hs=(0, 1)):
         on = "ev16" if i == 0 else "og%d" % i
@@ -325,16 +307,17 @@ def rank_program(g, core, T, topo):
         col = wcol(t, i - 1)
         ts(T["og%d" % i][:], PSM[:, col:col + 56], HALF + 0.2, None, A.add, None, [bank(col)], ["og%d" % i])
 
-    def off_s(t, i, part):
-        col = wcol(t, i - 1)
+    def off_s(t, i, part, n=1):
+        col, k = wcol(t, i - 1), 56 * n
+        bk = sorted({bank(col), bank(col + k - 1)})
         if part == 0:
-            ts(T.tB[:], PSM[:, col:col + 56], HALF / 8192.0 - HALF, 8192.0, A.add, A.mult, [bank(col)], ["tB"])
+            ts(T.tB[:, 0:k], PSM[:, col:col + k], HALF / 8192.0 - HALF, 8192.0, A.add, A.mult, bk, ["tB"])
         elif part == 1:
-            tt(T.mx[:], PSM[:, col:col + 56], T.tB[:], A.max, [bank(col), "tB"], ["mx"])
+            tt(T.mx[:, 0:k], PSM[:, col:col + k], T.tB[:, 0:k], A.max, bk + ["tB"], ["mx"])
         else:
-            ts(T["os%d" % i][:], T.mx[:], HALF + 0.2, None, A.add, None, ["mx"], ["os%d" % i])
+            ts(T.osb[:, 56 * i:56 * i + k], T.mx[:, 0:k], HALF + 0.2, None, A.add, None, ["mx"], ["os%d" % (i + j) for j in range(n)])
 
-    def diff(t, i, col):
+    def diff(t, i, col, part=None, hs=(0, 1)):
         if i == 0:
             terms = [("cBD", "mA0", 0), ("ncI", "mA0", 0), ("I14", "Pu", 0), ("BDn", "G0", 0)]
         elif i == 1:
@@ -345,7 +328,12 @@ def rank_program(g, core, T, topo):
             terms = [("BDm1", "G1", 0), ("BD1", "G3", 0)]
         else:
             terms = [("BDp", "G%d" % (i - 2), 0), ("BDn", "G%d" % i, 0)]
-        spread(col, terms)
+        if part == 0:
+            spread(col, terms[:-1], hs, last=False)
+        elif part == 1:
+            spread(col, terms[-1:], hs, first=False)
+        else:
+            spread(col, terms, hs)
 
     def times_s(i, col):
         if i % 2 == 0:
@@ -364,86 +352,92 @@ def rank_program(g, core, T, topo):
         tt(T.Lc[:, 0:WS].indirect(offs("os%d" % i, 0, (0, 1))), T["col%d" % i][:], T["upd%d" % i][:], A.add,
            ["os%d" % i] + hk("col%d" % i) + hk("upd%d" % i), LK)
 
+    def scat_u(h):
+        tt(T.Lc[:, 0:WS].indirect(offs("eu16", 0, (h,))), lanes("col6", (h,)), lanes("P0", (h,)), A.subtract,
+           ["eu16"] + hk("col6", (h,)) + hk("P0", (h,)), LK)
+
     rconv(0)
     rconv(1)
     rconv(2)
-    dma("s", "r1a", T.R1[:, 0:1536], T.R0[:, 0:1536], RK[0:3], ["R1.a"])
-    spread(PC, [("BDp", "X", 2 * E)])
     free_u(0, 0)
     free_u(0, 1)
+    rconv(3, True)
+    rconv(4, True)
     gather_col(6)
     for h in (0, 1):
         prefix("Fu", PB, h)
         mask_a(0, PB, h)
-    rconv(3, True)
-    rconv(4, True)
-    dma("s", "r1b", T.R1[:, 1536:W], T.R0[:, 1536:W], RK[3:5], ["R1.b"])
+    spread(PC, [("BDp", "X", 2 * E)])
     make_p(0, PA)
+    tt(T.Pu[:], PSM[:, PC:PC + E], T.mA0[:], A.mult, both(PC) + hk("mA0"), hk("Pu"))
+    dma("s", "r1a", T.R1[:, 0:1792], T.R0[:, 0:1792], RK[0:5], ["R1.a"])
+    scat_u(0)
+    rconv(6)
+    rconv(5)
+    dma("s", "r1b", T.R1[:, 1792:W], T.R0[:, 1792:W], RK[5:7], ["R1.b"])
+    diff(0, 0, PC, 0)
     free_v(0, 0)
     free_v(0, 1)
     walk(0, 0)
-    wrap(0, 0)
     for h in (0, 1):
         prefix("Fv", PB, h)
         mask_b(0, PB, h)
-    tt(T.Pu[:], PSM[:, PC:PC + E], T.mA0[:], A.mult, both(PC) + hk("mA0"), hk("Pu"))
+    wrap(0, 0)
+    scat_u(1)
     off_g(0, 1)
     off_s(0, 1, 0)
-    tt(T.Lc[:, 0:WS].indirect(offs("eu16", 0, (0, 1))), T.col6[:], T.P0[:], A.subtract, ["eu16"] + hk("col6") + hk("P0"), LK)
     make_s(0, PA)
+    diff(0, 0, PC, 1)
+    diff(0, 1, PB, 0)
     gather_col(0)
-    diff(0, 0, PB)
     gather_col(1)
-    off_s(0, 1, 1)
     walk(0, 1)
+    off_s(0, 1, 1)
     wrap(0, 1)
-    diff(0, 1, PC)
+    diff(0, 1, PB, 1)
+    diff(0, 2, PA, 0)
+    times_s(0, PC)
     off_s(0, 1, 2)
-    times_s(0, PB)
-    add_col(0, PB)
     off_g(0, 2)
-    off_s(0, 2, 0)
     gather_col(2)
-    scat_r(0)
+    add_col(0, PC)
     walk(0, 2)
     wrap(0, 2)
-    diff(0, 2, PA)
-    off_s(0, 2, 1)
-    times_s(1, PC)
-    off_s(0, 2, 2)
-    scat_l(1)
+    diff(0, 2, PA, 1)
+    colours(0, PC)
+    times_s(1, PB)
     off_g(0, 3)
-    off_s(0, 3, 0)
+    off_s(0, 2, 0, 2)
     gather_col(3)
+    scat_r(0)
+    diff(0, 3, PB, 0)
+    times_s(2, PA)
+    off_s(0, 2, 1, 2)
     walk(0, 3)
     wrap(0, 3)
-    diff(0, 3, PB)
-    colours(0, PC)
-    off_s(0, 3, 1)
-    times_s(2, PA)
-    off_s(0, 3, 2)
+    diff(0, 3, PB, 1)
+    off_s(0, 2, 2, 2)
     add_col(2, PA)
     off_g(0, 4)
-    off_s(0, 4, 0)
     gather_col(4)
+    diff(0, 4, PC, 0)
     diff(0, 5, PA)
+    scat_l(1)
     walk(0, 4)
     wrap(0, 4)
-    diff(0, 4, PC)
-    off_s(0, 4, 1)
+    diff(0, 4, PC, 1)
     times_s(3, PB)
-    off_s(0, 4, 2)
     off_g(0, 5)
-    off_s(0, 5, 0)
+    off_s(0, 4, 0, 2)
     gather_col(5)
     scat_r(2)
-    times_s(5, PA)
-    off_s(0, 5, 1)
     times_s(4, PC)
-    off_s(0, 5, 2)
+    off_s(0, 4, 1, 2)
     add_col(4, PC)
+    off_s(0, 4, 2, 2)
     scat_r(4)
     scat_l(3)
+    times_s(5, PA)
     free_v(1, 0)
     free_v(1, 1)
     for h in (0, 1):
@@ -459,9 +453,11 @@ def rank_program(g, core, T, topo):
             tt(T.DL[:, 0:WS].indirect(offs("os%d" % i, 1, hs)), lanes("upd%d" % i, hs), lanes("S1", hs), A.mult,
                ["os%d" % i] + hk("upd%d" % i, hs) + hk("S1", hs), ["DL"])
 
-    def diff_out(i):
-        diff(1, i, PC)
-        act(T["upd%d" % i][:], PSM[:, PC:PC + E], F.Copy, both(PC), hk("upd%d" % i))
+    def diff_out(i, part=None):
+        for h in (0, 1):
+            a, b = HV[h]
+            diff(1, i, PC, part, (h,))
+            act(lanes("upd%d" % i, (h,)), PSM[:, PC + a:PC + b], F.Copy, [bank(PC + a)], hk("upd%d" % i, (h,)))
 
     free_u(1, 0)
     free_u(1, 1)
@@ -473,38 +469,40 @@ def rank_program(g, core, T, topo):
     make_p(1, PA)
     wrap(1, 0)
     make_s(1, PB)
+    diff(1, 1, PC, 0)
     scat_d(6, (0,))
     off_g(1, 1)
     off_s(1, 1, 0)
     walk(1, 1)
     off_s(1, 1, 1)
     wrap(1, 1)
-    diff_out(1)
+    diff_out(1, 1)
     colours(1, PB)
     for b in range(5):
         act(PSM[:, 512 * b:512 * b + 512], T.Lc[:, 512 * b:512 * b + 512], F.Identity, LK, [bank(512 * b)], bias=float(HALF))
     scat_d(6, (1,))
-    off_s(1, 1, 2)
     off_g(1, 2)
+    off_s(1, 1, 2)
     walk(1, 2)
     wrap(1, 2)
+    diff(1, 3, PC, 0)
     scat_d(1, (0,))
     off_g(1, 3)
     off_s(1, 3, 0)
     walk(1, 3)
     off_s(1, 3, 1)
     wrap(1, 3)
-    diff_out(3)
+    diff_out(3, 1)
     scat_d(1, (1,))
-    off_s(1, 3, 2)
     off_g(1, 4)
+    off_s(1, 3, 2)
     walk(1, 4)
     wrap(1, 4)
     diff_out(5)
     scat_d(3, (0,))
     off_s(1, 5, 0)
-    scat_d(3, (1,))
     off_s(1, 5, 1)
+    scat_d(3, (1,))
     off_s(1, 5, 2)
     scat_d(5, (0, 1))
     for b in range(5):

from concourse.mybir import AluOpType, ActivationFunctionType

W, E = 2560, 896
HALF = W // 2
WG, WS = W + 8, W + E + 8
SG = 2.0 ** -17
RCH = [(0, 256), (256, 1024), (1024, 1792), (1792, 2560)]
RP = [(0, 256, 0), (256, 640, 1), (640, 1024, 1), (1024, 1408, 2), (1408, 1792, 2), (1792, 2176, 3), (2176, 2560, 3)]
LCH = [(0, 1024), (1024, 2048), (2048, 2560)]
HV = [(0, 512), (512, 896)]
SCRATCH = {"PSM": ("psum", [128, 4096], "float32")}
for _d, _l in (
        ("int32", [("rti", W), ("lti", W), ("eui", 112), ("evi", 112), ("qi", 1), ("si", 1)]),
        ("uint16", [("eu16", 112), ("ev16", 112), ("osb", 336)] + [("og%d" % i, 56) for i in range(1, 6)]),
        ("float16", [("r16", W), ("rl16", W), ("wv", 168), ("X", 3 * E), ("Pu", E), ("Jf", 56)] + [("G%d" % i, E) for i in range(5)]),
        ("bfloat16", [("E1", 144), ("E8", 144), ("Cw", 8)]
         + [(n, 128) for n in ("BD1", "BDm1", "BDp", "BDn", "I14", "Ib2", "Ibm1", "Wd5", "cBD", "ncI", "Pfn")]
         + [(n, E) for n in ("Fu", "Fv", "mA0", "mA1", "mB0", "mB1")]),
        ("float32", [("Lc", WS), ("R0", WG), ("R1", WS), ("DL", WS), ("Yo", W), ("yas", 2 * E), ("TT", 144), ("GP", 128),
                     ("PS16", 128), ("Jb", 56), ("sel", 16), ("tl", 128), ("Low", 128), ("tB", 112), ("mx", 112)]
         + [(n, 1) for n in ("qf", "sf", "g16", "s14", "bB")] + [(n, E) for n in ("S0", "S1", "P0", "P1")]
         + [("col%d" % i, E) for i in range(7)] + [("upd%d" % i, E) for i in range(6)])):
    for _n, _c in _l:
        SCRATCH[_n] = ("sbuf", [128, _c], _d)

QSEM = {"g": "cg", "v": "cv", "a": "ca", "p": "cp"}
DMAS = (["eu", "ev", "r1a", "r1b", "ya0", "ya1"] + ["rt%d" % c for c in range(len(RCH))] + ["lt%d" % c for c in range(len(LCH))]
        + ["y%d" % b for b in range(5)])
SEMAPHORES = list(QSEM.values()) + ["d_" + n for n in DMAS] + ["arr%d" % c for c in range(len(RCH))] + ["sent"]
PA, PB, PW0, PC = 0, 1024, 2560, 3072


def bank(col):
    return "B%d" % (col // 512)


def emit(ops, queues, T):
    last_w, readers, known, waits, marked = {}, {}, {}, [], set()
    for n, o in enumerate(ops):
        deps = set()
        for k in o["r"]:
            if k in last_w:
                deps.add(last_w[k])
            if k[0] == "B" and len(k) == 2:
                deps.update(m for m in readers.get(k, []) if ops[m]["q"] != o["q"])
        for k in o["w"]:
            if k in last_w:
                deps.add(last_w[k])
            deps.update(readers.get(k, []))
        best = {}
        for m in deps:
            p = ops[m]
            if p["q"] == "p" and o["q"] == "p":
                continue
            src = p["sem"] if p["sem"] else p["q"]
            best[src] = max(best.get(src, -1), m)
        mine = []
        if o["q"] is not None:
            for src in sorted(best):
                m = best[src]
                if known.get((o["q"], src), -1) < m:
                    known[(o["q"], src)] = m
                    mine.append(m)
                    marked.add(m)
        waits.append(mine)
        for k in o["r"]:
            readers.setdefault(k, []).append(n)
        for k in o["w"]:
            last_w[k] = n
            readers[k] = []
    count, value = {}, {}
    for n, o in enumerate(ops):
        if o["sem"]:
            value[n] = (o["sem"], o["n"])
        elif n in marked:
            count[o["q"]] = count.get(o["q"], 0) + 1
            value[n] = (QSEM[o["q"]], count[o["q"]])
    for n, o in enumerate(ops):
        if o["q"] is None:
            continue
        q = queues[o["q"]]
        for m in waits[n]:
            q.wait_ge(T.sem[value[m][0]], value[m][1])
        if o["f"] is None:
            continue
        ins = o["f"]()
        if o["sem"]:
            ins.then_inc(T.sem[o["sem"]], o["n"])
        elif n in marked:
            ins.then_inc(T.sem[value[n][0]], 1)


def rank_program(g, core, T, topo):
    rank = T.rank_of(core)
    if rank is None:
        return
    A, F = AluOpType, ActivationFunctionType
    V, SC, PE = g.vector, g.scalar, g.tensor
    N = len(T.cores)
    dst = T.cores[(rank - 1) % N]
    src = T.cores[(rank + 1) % N]
    rid, pid = topo.addr(dst)[0], topo.addr(dst)[1]
    n_out, n_in = len(topo.engines(core, dst)), len(topo.engines(src, core))
    PSM = T.PSM
    ops = []

    def op(q, f, r, w, sem=None, n=0):
        ops.append({"q": q, "f": f, "r": list(r), "w": list(w), "sem": sem, "n": n})

    def dma(q, name, out, in_, r, w):
        eng = {"s": g.sync, "a": g.scalar}[q]
        op(q, lambda: eng.dma_start(out, in_), r, w, "d_" + name, 16)

    def ts(out, in0, s1, s2, o0, o1, r, w):
        if s2 is None:
            op("v", lambda: V.tensor_scalar(out, in0, s1, None, o0), r, w)
        else:
            op("v", lambda: V.tensor_scalar(out, in0, s1, s2, o0, o1), r, w)

    def tt(out, in0, in1, o, r, w):
        op("v", lambda: V.tensor_tensor(out, in0, in1, o), r, w)

    def act(out, in_, func, r, w, bias=None, scale=None):
        kw = {}
        if bias is not None:
            kw["bias"] = bias
        if scale is not None:
            kw["scale"] = scale
        op("a", lambda: SC.activation(out, in_, func, **kw), r, w)

    def mm(out, col, terms, first=True, last=True):
        for i, (lh, lk, rh, rk) in enumerate(terms):
            st, sp = first and i == 0, last and i == len(terms) - 1
            op("p", lambda lh=lh, rh=rh, st=st, sp=sp: PE.matmul(out, lh, rh, st, sp), [lk] + list(rk), [bank(col)])

    def hk(name, hs=(0, 1)):
        return [name + "." + str(h) for h in hs]

    def both(col):
        return [bank(col), bank(col + 512)]

    def spread(col, terms, hs=(0, 1), rows=128, first=True, last=True):
        for h in hs:
            a, b = HV[h]
            mm(PSM[0:rows, col + a:col + b], col + a,
               [(T[wn][:], wn, T[bn][:, c0 + a:c0 + b], XK if bn == "X" else hk(bn, (h,))) for wn, bn, c0 in terms], first, last)

    def offs(name, t, hs):
        c0 = 56 * t if name in ("eu16", "ev16") else 0
        if name[:2] == "os":
            name, c0 = "osb", 56 * int(name[2])
        return T[name][:, c0 + HV[hs[0]][0] // 16:c0 + HV[hs[-1]][1] // 16]

    def lanes(name, hs):
        return T[name][:, HV[hs[0]][0]:HV[hs[-1]][1]]

    RK = ["R0.%d" % b for b in range(len(RP))] + ["R0.n"]
    R1K = ["R1.a", "R1.b", "R1.n"]
    LK = ["Lc.%d" % c for c in range(len(LCH))] + ["Lc.n"]
    XK = ["X%d" % s for s in range(16)]

    def rtab(t):
        return (T.R0, RK) if t == 0 else (T.R1, R1K)

    dma("a", "ev", T.evi[:], T.ev[:], [], ["evi"])
    dma("a", "eu", T.eui[:], T.eu[:], [], ["eui"])
    for c, (a, b) in enumerate(RCH):
        dma("s", "rt%d" % c, T.rti[:, a:b], T.rt[:, a:b], [], ["rti.%d" % c])
    for c, (a, b) in enumerate(LCH):
        dma("s", "lt%d" % c, T.lti[:, a:b], T.lt[:, a:b], [], ["lti.%d" % c])

    def iota(name, out, pattern, base, cm, flag=True):
        if flag:
            op("g", lambda: g.iota(out, pattern, base, cm, allow_small_or_imprecise_dtypes=True), [], [name])
        else:
            op("g", lambda: g.iota(out, pattern, base, cm), [], [name])

    iota("qi", T.qi[:], [[0, 1]], 0, 1, False)
    iota("qf", T.qf[:], [[0, 1]], 0, 1)
    iota("TT", T.TT[:], [[1, 144]], -15, 0)
    iota("PS16", T.PS16[:], [[0, 8], [1, 16]], 0, 0)
    iota("GP", T.GP[:], [[16, 8], [0, 16]], 0, 0)
    iota("Jb", T.Jb[:], [[16, 56]], 1, 0)
    iota("Lc.n", T.Lc[:, W:WG], [[0, 8]], HALF, 0)
    for c in range(len(RCH)):
        op(None, None, [], ["rl16.%d" % c], "arr%d" % c, n_in)

    def send(c):
        a, b = RCH[c]
        ts(T.r16[:, a:b], T.rti[:, a:b], -float(HALF), None, A.add, None, ["rti.%d" % c], ["r16.%d" % c])
        op("g", lambda: g.remote_dma(T.rl16[:, a:b], T.r16[:, a:b], T.sem["arr%d" % c], T.sem.sent, pid, rid,
                                     topo.mask(core, dst)), ["r16.%d" % c], [])

    ts(T.si[:], T.qi[:], 15, None, A.bitwise_and, None, ["qi"], ["si"])
    op("v", lambda: V.tensor_copy(T.sf[:], T.si[:]), ["si"], ["sf"])
    tt(T.g16[:], T.qf[:], T.sf[:], A.subtract, ["qf", "sf"], ["g16"])
    ts(T.Ibm1[:], T.TT[:, 15:143], T.qf[:], -1.0, A.is_equal, A.mult, ["TT", "qf"], ["Ibm1"])
    ts(T.E1[:], T.TT[:], T.g16[:], None, A.is_equal, None, ["TT", "g16"], ["E1"])
    act(T.s14[:], T.sf[:], F.Copy, ["sf"], ["s14"], scale=2.0 ** -14)
    act(T.bB[:], T.sf[:], F.Identity, ["sf"], ["bB"], bias=0.5, scale=-0.5)
    ts(T.sel[:], T.PS16[:, 0:16], T.sf[:], None, A.is_equal, None, ["PS16", "sf"], ["sel"])
    ts(T.tl[:], T.PS16[:], T.sf[:], None, A.is_gt, None, ["PS16", "sf"], ["tl"])
    ts(T.BD1[:], T.GP[:], T.g16[:], None, A.is_equal, None, ["GP", "g16"], ["BD1"])
    ts(T.Cw[:], T.GP[:, 0:128:16], T.g16[:], T.s14[:], A.is_equal, A.mult, ["GP", "g16", "s14"], ["Cw"])
    send(0)
    for name, base, val in (("I14", "Ibm1", -2.0 ** -14), ("Ib2", "Ibm1", -0.25), ("ncI", "Ibm1", HALF * 2.0 ** -31),
                            ("E8", "E1", 8.0), ("Wd5", "BD1", float(HALF)), ("BDm1", "BD1", -1.0), ("BDp", "BD1", 2.0 ** -14),
                            ("BDn", "BD1", -2.0 ** -14), ("cBD", "BD1", HALF * 2.0 ** -31)):
        act(T[name][:], T[base][:], F.Copy, [base], [name], scale=val)
    act(T.R0[:, W:WG], T.Lc[:, W:WG], F.Copy, ["Lc.n"], ["R0.n"], scale=SG)
    act(T.R1[:, W:WG], T.Lc[:, W:WG], F.Copy, ["Lc.n"], ["R1.n"], scale=SG)
    tt(T.Low[:], T.tl[:], T.BD1[:], A.mult, ["tl", "BD1"], ["Low"])
    ts(T.Jf[:], T.Jb[:], T.sf[:], 2.0, A.add, A.mult, ["Jb", "sf"], ["Jf"])
    op("v", lambda: V.tensor_copy(T.ev16[:], T.evi[:]), ["evi"], ["ev16"])
    op("v", lambda: V.tensor_copy(T.eu16[:], T.eui[:]), ["eui"], ["eu16"])
    ts(T.wv[:, 0:112], T.evi[:], -float(HALF), -1.0, A.add, A.mult, ["evi"], ["wv.0"])
    ts(T.wv[:, 112:168], T.eui[:, 0:56], -float(HALF), 0.125, A.add, A.mult, ["eui"], ["wv.1"])
    tt(T.Pfn[:], T.Low[:], T.Ibm1[:], A.add, ["Low", "Ibm1"], ["Pfn"])

    def xpart(s0, s1):
        for s in range(s0, s1):
            ts(T.X[:, s:3 * E:16], T.wv[:], T.sel[:, s:s + 1], None, A.mult, None, ["wv.0", "wv.1", "sel"], ["X%d" % s])

    send(1)
    xpart(0, 5)
    send(2)
    xpart(5, 10)
    send(3)
    xpart(10, 13)
    iota("DL", T.DL[:, 0:W], [[0, W]], 0, 0)
    for c, (a, b) in enumerate(LCH):
        ts(T.Lc[:, a:b], T.lti[:, a:b], -float(HALF), None, A.add, None, ["lti.%d" % c], ["Lc.%d" % c])
    xpart(13, 16)

    def rconv(b, on_vector=False):
        x, y, c = RP[b]
        sl = slice(x, y)
        if on_vector:
            ts(T.R0[:, sl], T.rl16[:, sl], SG, None, A.mult, None, ["rl16.%d" % c], ["R0.%d" % b])
        else:
            col = (PA if b < 5 else PB) + 512 * (b % 2)
            mm(PSM[:, col:col + y - x], col, [(T.I14[:], "I14", T.rl16[:, sl], ["rl16.%d" % c])])
            act(T.R0[:, sl], PSM[:, col:col + y - x], F.Copy, [bank(col)], ["R0.%d" % b], scale=0.125)

    def prefix(fb, col, h):
        spread(col, [("Pfn", fb, 0)], (h,))

    def mask_a(t, col, h):
        a, b = HV[h]
        act(lanes("mA%d" % t, (h,)), PSM[:, col + a:col + b], F.Relu, [bank(col + a)], hk("mA%d" % t, (h,)), scale=-16384.0)

    def mask_b(t, col, h):
        a, b = HV[h]
        act(lanes("mB%d" % t, (h,)), PSM[:, col + a:col + b], F.Relu, [bank(col + a), "bB"], hk("mB%d" % t, (h,)),
            bias=T.bB[:], scale=-0.5)

    def free_u(t, h):
        ts(lanes("Fu", (h,)), T.Lc[:, 0:WG].indirect(offs("eu16", t, (h,))), HALF - 0.5, None, A.is_ge, None,
           LK + ["eu16"], hk("Fu", (h,)))

    def free_v(t, h):
        tab, keys = rtab(t)
        act(lanes("Fv", (h,)), tab[:, 0:WG].indirect(offs("ev16", t, (h,))), F.Sign, keys + ["ev16"], hk("Fv", (h,)),
            bias=0.5 - HALF, scale=1.0 / SG)

    def make_p(t, col):
        for h in (0, 1):
            a, b = HV[h]
            spread(col, [("BD1", "X", t * E), ("Ib2", "mA%d" % t, 0)], (h,))
            act(lanes("P%d" % t, (h,)), PSM[:, col + a:col + b], F.Relu, [bank(col + a)], hk("P%d" % t, (h,)),
                bias=float(HALF - 4096))

    def make_s(t, col):
        for h in (0, 1):
            a, b = HV[h]
            spread(col, [("Ib2", "mA%d" % t, 0), ("Ibm1", "mB%d" % t, 0)], (h,))
            act(lanes("S%d" % t, (h,)), PSM[:, col + a:col + b], F.Sign, [bank(col + a)], hk("S%d" % t, (h,)))

    def colours(t, col):
        spread(col, [("Cw", "mA%d" % t, 0)], rows=8)
        act(T.yas[0:8, t * E:(t + 1) * E], PSM[0:8, col:col + E], F.Copy, both(col), ["yas%d" % t])
        dma("s", "ya%d" % t, T.ya[:, t * E:(t + 1) * E], T.yas[0:8, t * E:(t + 1) * E], ["yas%d" % t], ["out.ya%d" % t])

    def gather_col(i, t=0):
        on = "eu16" if i == 6 else ("ev16" if i == 0 else "og%d" % i)
        tab, keys = rtab(t) if i in (0, 2, 4) else (T.Lc, LK)
        act(T["col%d" % i][:], tab[:, 0:WG].indirect(offs(on, t, (0, 1))), F.Copy, keys + [on], hk("col%d" % i))

    def wcol(t, i):
        return PW0 - 56 if t == 0 and i % 2 else PW0

    def walk(t, i, hs=(0, 1)):
        on = "ev16" if i == 0 else "og%d" % i
        tab, keys = rtab(t) if i % 2 == 0 else (T.Lc, LK)
        mk = ("mA%d" if i % 2 == 0 else "mB%d") % t
        tt(lanes("G%d" % i, hs), tab[:, 0:WG].indirect(offs(on, t, hs)), lanes(mk, hs), A.mult,
           keys + [on] + hk(mk, hs), hk("G%d" % i, hs))

    def wrap(t, i):
        col = wcol(t, i)
        en = "E8" if i % 2 == 0 else "E1"
        terms = [(T.I14[:], "I14", T.Jf[:], ["Jf"])]
        terms += [(T[en][:, 15 - s:143 - s], en, T["G%d" % i][:, s:E:16], hk("G%d" % i)) for s in range(16)]
        mm(PSM[:, col:col + 56], col, terms)

    def off_g(t, i):
        col = wcol(t, i - 1)
        ts(T["og%d" % i][:], PSM[:, col:col + 56], HALF + 0.2, None, A.add, None, [bank(col)], ["og%d" % i])

    def off_s(t, i, part, n=1):
        col, k = wcol(t, i - 1), 56 * n
        bk = sorted({bank(col), bank(col + k - 1)})
        if part == 0:
            ts(T.tB[:, 0:k], PSM[:, col:col + k], HALF / 8192.0 - HALF, 8192.0, A.add, A.mult, bk, ["tB"])
        elif part == 1:
            tt(T.mx[:, 0:k], PSM[:, col:col + k], T.tB[:, 0:k], A.max, bk + ["tB"], ["mx"])
        else:
            ts(T.osb[:, 56 * i:56 * i + k], T.mx[:, 0:k], HALF + 0.2, None, A.add, None, ["mx"], ["os%d" % (i + j) for j in range(n)])

    def diff(t, i, col, part=None, hs=(0, 1)):
        if i == 0:
            terms = [("cBD", "mA0", 0), ("ncI", "mA0", 0), ("I14", "Pu", 0), ("BDn", "G0", 0)]
        elif i == 1:
            terms = [("BD1", "X", t * E), ("BD1", "G1", 0)]
        elif i == 5:
            terms = [("Wd5", "mB%d" % t, 0), ("BDm1", "G3", 0)]
        elif i == 3:
            terms = [("BDm1", "G1", 0), ("BD1", "G3", 0)]
        else:
            terms = [("BDp", "G%d" % (i - 2), 0), ("BDn", "G%d" % i, 0)]
        if part == 0:
            spread(col, terms[:-1], hs, last=False)
        elif part == 1:
            spread(col, terms[-1:], hs, first=False)
        else:
            spread(col, terms, hs)

    def times_s(i, col):
        if i % 2 == 0:
            tt(PSM[:, col:col + E], PSM[:, col:col + E], T.S0[:], A.mult, both(col) + hk("S0"), both(col))
        else:
            tt(T["upd%d" % i][:], PSM[:, col:col + E], T.S0[:], A.mult, both(col) + hk("S0"), hk("upd%d" % i))

    def add_col(i, col):
        tt(T["upd%d" % i][:], PSM[:, col:col + E], T["col%d" % i][:], A.add, both(col) + hk("col%d" % i), hk("upd%d" % i))

    def scat_r(i):
        on = "ev16" if i == 0 else "os%d" % i
        act(T.R1[:, 0:WS].indirect(offs(on, 0, (0, 1))), T["upd%d" % i][:], F.Tanh, [on] + hk("upd%d" % i), R1K)

    def scat_l(i):
        tt(T.Lc[:, 0:WS].indirect(offs("os%d" % i, 0, (0, 1))), T["col%d" % i][:], T["upd%d" % i][:], A.add,
           ["os%d" % i] + hk("col%d" % i) + hk("upd%d" % i), LK)

    def scat_u(h):
        tt(T.Lc[:, 0:WS].indirect(offs("eu16", 0, (h,))), lanes("col6", (h,)), lanes("P0", (h,)), A.subtract,
           ["eu16"] + hk("col6", (h,)) + hk("P0", (h,)), LK)

    rconv(0)
    rconv(1)
    rconv(2)
    free_u(0, 0)
    free_u(0, 1)
    rconv(3, True)
    rconv(4, True)
    gather_col(6)
    for h in (0, 1):
        prefix("Fu", PB, h)
        mask_a(0, PB, h)
    spread(PC, [("BDp", "X", 2 * E)])
    make_p(0, PA)
    tt(T.Pu[:], PSM[:, PC:PC + E], T.mA0[:], A.mult, both(PC) + hk("mA0"), hk("Pu"))
    dma("s", "r1a", T.R1[:, 0:1792], T.R0[:, 0:1792], RK[0:5], ["R1.a"])
    scat_u(0)
    rconv(6)
    rconv(5)
    dma("s", "r1b", T.R1[:, 1792:W], T.R0[:, 1792:W], RK[5:7], ["R1.b"])
    diff(0, 0, PC, 0)
    free_v(0, 0)
    free_v(0, 1)
    walk(0, 0)
    for h in (0, 1):
        prefix("Fv", PB, h)
        mask_b(0, PB, h)
    wrap(0, 0)
    scat_u(1)
    off_g(0, 1)
    off_s(0, 1, 0)
    make_s(0, PA)
    diff(0, 0, PC, 1)
    diff(0, 1, PB, 0)
    gather_col(0)
    gather_col(1)
    walk(0, 1)
    off_s(0, 1, 1)
    wrap(0, 1)
    diff(0, 1, PB, 1)
    diff(0, 2, PA, 0)
    times_s(0, PC)
    off_s(0, 1, 2)
    off_g(0, 2)
    gather_col(2)
    add_col(0, PC)
    walk(0, 2)
    wrap(0, 2)
    diff(0, 2, PA, 1)
    colours(0, PC)
    times_s(1, PB)
    off_g(0, 3)
    off_s(0, 2, 0, 2)
    gather_col(3)
    scat_r(0)
    diff(0, 3, PB, 0)
    times_s(2, PA)
    off_s(0, 2, 1, 2)
    walk(0, 3)
    wrap(0, 3)
    diff(0, 3, PB, 1)
    off_s(0, 2, 2, 2)
    add_col(2, PA)
    off_g(0, 4)
    gather_col(4)
    diff(0, 4, PC, 0)
    diff(0, 5, PA)
    scat_l(1)
    walk(0, 4)
    wrap(0, 4)
    diff(0, 4, PC, 1)
    times_s(3, PB)
    off_g(0, 5)
    off_s(0, 4, 0, 2)
    gather_col(5)
    scat_r(2)
    times_s(4, PC)
    off_s(0, 4, 1, 2)
    add_col(4, PC)
    off_s(0, 4, 2, 2)
    scat_r(4)
    scat_l(3)
    times_s(5, PA)
    free_v(1, 0)
    free_v(1, 1)
    for h in (0, 1):
        prefix("Fv", PC, h)
        mask_b(1, PC, h)
    scat_l(5)

    def scat_d(i, hs):
        if i == 6:
            ts(T.DL[:, 0:WS].indirect(offs("eu16", 1, hs)), lanes("P1", hs), -1.0, 0.0, A.mult, A.add,
               ["eu16"] + hk("P1", hs), ["DL"])
        else:
            tt(T.DL[:, 0:WS].indirect(offs("os%d" % i, 1, hs)), lanes("upd%d" % i, hs), lanes("S1", hs), A.mult,
               ["os%d" % i] + hk("upd%d" % i, hs) + hk("S1", hs), ["DL"])

    def diff_out(i, part=None):
        for h in (0, 1):
            a, b = HV[h]
            diff(1, i, PC, part, (h,))
            act(lanes("upd%d" % i, (h,)), PSM[:, PC + a:PC + b], F.Copy, [bank(PC + a)], hk("upd%d" % i, (h,)))

    free_u(1, 0)
    free_u(1, 1)
    for h in (0, 1):
        prefix("Fu", PB, h)
        mask_a(1, PB, h)
    walk(1, 0, (0,))
    walk(1, 0, (1,))
    make_p(1, PA)
    wrap(1, 0)
    make_s(1, PB)
    diff(1, 1, PC, 0)
    scat_d(6, (0,))
    off_g(1, 1)
    off_s(1, 1, 0)
    walk(1, 1)
    off_s(1, 1, 1)
    wrap(1, 1)
    diff_out(1, 1)
    colours(1, PB)
    for b in range(5):
        act(PSM[:, 512 * b:512 * b + 512], T.Lc[:, 512 * b:512 * b + 512], F.Identity, LK, [bank(512 * b)], bias=float(HALF))
    scat_d(6, (1,))
    off_g(1, 2)
    off_s(1, 1, 2)
    walk(1, 2)
    wrap(1, 2)
    diff(1, 3, PC, 0)
    scat_d(1, (0,))
    off_g(1, 3)
    off_s(1, 3, 0)
    walk(1, 3)
    off_s(1, 3, 1)
    wrap(1, 3)
    diff_out(3, 1)
    scat_d(1, (1,))
    off_g(1, 4)
    off_s(1, 3, 2)
    walk(1, 4)
    wrap(1, 4)
    diff_out(5)
    scat_d(3, (0,))
    off_s(1, 5, 0)
    off_s(1, 5, 1)
    scat_d(3, (1,))
    off_s(1, 5, 2)
    scat_d(5, (0, 1))
    for b in range(5):
        sl = slice(512 * b, 512 * b + 512)
        tt(T.Yo[:, sl], PSM[:, sl], T.DL[:, sl], A.add, [bank(512 * b), "DL"], ["Yo%d" % b])
        dma("s" if b % 2 == 0 else "a", "y%d" % b, T.yl[:, sl], T.Yo[:, sl], ["Yo%d" % b], ["out.y%d" % b])
    op("s", None, ["out.y%d" % b for b in range(5)] + ["out.ya0", "out.ya1"], [])

    emit(ops, {"g": g, "v": V, "a": SC, "p": PE, "s": g.sync}, T)
    g.wait_ge(T.sem.sent, n_out * len(RCH))
